import numpy as np, ml_dtypes
CORES = [14,30,46,142,158,174,270,286,302,398,414,430]
N = 12
import mx_ref
NC, G = 128, 2
C = np.float32(0.043)
BF = ml_dtypes.bfloat16
def cut(t, i, w=512):
    return t[:, w * i:w * i + w]
def tile(rs):
    return np.stack(rs, axis=2).reshape(128, -1).astype(BF)
def fold(P):
    return [f(p, axis=0) * C for p in P for f in (np.max, np.min)]
def setup_inputs(rng):
    def f(*shape):
        return mx_ref.flush((rng.standard_normal(shape, dtype=np.float32) * np.exp2(rng.integers(-2, 3, shape[:-1] + (1,)))).astype(BF))
    return {"x": f(N, 128, 4 * NC), "w1": f(N, 128, G * 512), "w2": f(N, 128, 2 * 512)}
def setup_inputs_blocks(rng):
    d = setup_inputs(rng)
    for k in ("x", "w1", "w2"): d[k] = mx_ref.spread(d[k], rng, 4)
    return d
def setup_inputs_wide(rng):
    d = setup_inputs(rng)
    for k in ("x", "w1", "w2"): d[k] = mx_ref.flush((d[k].astype(np.float32) * np.exp2(rng.integers(-8, 9, (N, 1, 1))).astype(np.float32)).astype(BF))
    return d
def reference(x, w1, w2, own=None):
    X = [mx_ref.quantize(x[j]) for j in range(N)]
    h = np.stack([tile(fold([[mx_ref.matmul(mx_ref.quantize(cut(w1[r], i)), X[j]) for j in range(N)] for i in range(G)])) for r in range(N)])
    use = h if own is None else own["h"]
    H = [mx_ref.quantize(use[j]) for j in range(N)]
    y = np.zeros((N, 128, NC), np.float32)
    for r in range(N):
        y[r] = mx_ref.matmul(mx_ref.quantize(cut(w2[r], 0)), H[r]) + mx_ref.matmul(mx_ref.quantize(cut(w2[r], 1)), H[(r + 1) % N])
    return {"h": h, "y": y}

@@ -1,0 +1,197 @@
+from concourse.bass import DstId, RemoteDMATransfer
+from concourse.mybir import dt, AluOpType, ActivationFunctionType
+
+N = 12
+NC = 128
+WORLD = 512
+SCALE = 0.043
+USE_HELPER = False
+
+SCRATCH = {
+    "xb": ("sbuf", [128, 512], "bfloat16"),
+    "w1b": ("sbuf", [128, 1024], "bfloat16"),
+    "w2b": ("sbuf", [128, 1024], "bfloat16"),
+    "xq": ("sbuf", [128, N * NC], "float8_e4m3fn_x4"),
+    "xs": ("sbuf", [128, N * NC], "uint8"),
+    "w1q": ("sbuf", [128, 256], "float8_e4m3fn_x4"),
+    "w1s": ("sbuf", [128, 256], "uint8"),
+    "w2q": ("sbuf", [128, 256], "float8_e4m3fn_x4"),
+    "w2s": ("sbuf", [128, 256], "uint8"),
+    "hb": ("sbuf", [128, 512], "bfloat16"),
+    "hq": ("sbuf", [128, 256], "float8_e4m3fn_x4"),
+    "hs": ("sbuf", [128, 256], "uint8"),
+    "seed": ("sbuf", [128, 256], "float32"),
+    "run": ("sbuf", [128, 512], "float32"),
+    "yb": ("sbuf", [128, 128], "float32"),
+    "ps": ("psum", [128, 512 * 7], "float32"),
+}
+SEMAPHORES = (["ldx", "ldw1", "ldw2", "qx", "qw1", "qw2", "qh", "arh", "left", "lefth", "seed0", "seed1",
+               "ch0", "ch1", "ch2", "ch3", "sc", "my", "cy", "sth", "sty"]
+              + ["ar%d" % j for j in range(N)]
+              + ["mm%d_%d" % (k, i) for k in range(N) for i in range(2)])
+
+
+def _bits(m):
+    return bin(m).count("1")
+
+
+def _plan(T, topo):
+    cores = list(T.cores)
+    plan = {}
+    for r, s in enumerate(cores):
+        rack = [c for c in cores if topo.rack(topo.host(c)) == topo.rack(topo.host(s))]
+        a, n = rack.index(s), len(rack)
+        partner = [c for c in cores if topo.rack(topo.host(c)) != topo.rack(topo.host(s))
+                   and topo.may_write(s, c) and topo.chip(c) == topo.chip(s)][0]
+        relay = s
+        if USE_HELPER:
+            relay = [c for c in range(WORLD) if topo.host(c) == topo.host(s) and topo.chip(c) == topo.chip(s)
+                     and topo.die(c) != topo.die(s)][0]
+        plan[s] = {"rank": r, "partner": partner, "relay": relay,
+                   "serve": [rack[(a + k) % n] for k in range(1, n)],
+                   "from": [rack[(a - k) % n] for k in range(1, n)]}
+    return plan
+
+
+def _send(g, T, topo, core, qbuf, sbuf, src_col, dst_col, width, dests, rsem, lsem):
+    mask = topo.mask(core, dests[0])
+    for d in dests:
+        mask &= topo.mask(core, d)
+    ids = []
+    for d in dests:
+        rid, pid = topo.addr(d, core)
+        ids.append(DstId(rid=rid, pnc=pid))
+    for kind in range(2):
+        if kind == 0:
+            src = T[qbuf][:, src_col:src_col + width].bitcast(dt.uint8)
+            dst = [T[qbuf][:, dst_col:dst_col + width].bitcast(dt.uint8) for _ in dests]
+        else:
+            src = T[sbuf][:, src_col:src_col + width]
+            dst = [T[sbuf][:, dst_col:dst_col + width] for _ in dests]
+        g.remote_dma_fused([RemoteDMATransfer(dst_ids=ids, dma_engine_mask=mask, remote_sem=T.sem[rsem],
+                                              srcs=[src], dsts=dst)], local_sem=T.sem[lsem])
+    return _bits(mask)
+
+
+def rank_program(g, core, T, topo):
+    plan = _plan(T, topo)
+    cores = list(T.cores)
+    rank = T.rank_of(core)
+    S = T.sem
+
+    if rank is None:
+        for s in cores:
+            p = plan[s]
+            if p["relay"] == core:
+                j = plan[p["partner"]]["rank"]
+                g.wait_ge(S["ar%d" % j], 2 * _bits(topo.mask(p["partner"], core)))
+                e = _send(g, T, topo, core, "xq", "xs", j * NC, j * NC, NC, p["serve"], "ar%d" % j, "left")
+                g.wait_ge(S.left, 2 * e)
+        return
+
+    me = plan[core]
+    pj = plan[me["partner"]]["rank"]
+    own = rank * NC
+
+    def arrives(j):
+        src = cores[j]
+        if src == me["partner"] or topo.rack(topo.host(src)) == topo.rack(topo.host(core)):
+            return 2 * _bits(topo.mask(src, core))
+        return 2 * _bits(topo.mask(plan[plan[src]["partner"]]["relay"], core))
+
+    g.sync.dma_start(T.xb[:], T.x[:]).then_inc(S.ldx, 16)
+    g.sync.dma_start(T.w1b[:], T.w1[:]).then_inc(S.ldw1, 16)
+
+    g.wait_ge(S.qx, 1)
+    left = 0
+    if USE_HELPER:
+        left += 2 * _send(g, T, topo, core, "xq", "xs", own, own, NC, [plan[me["partner"]]["relay"]], "ar%d" % rank, "left")
+        left += 2 * _send(g, T, topo, core, "xq", "xs", own, own, NC, me["serve"] + [me["partner"]], "ar%d" % rank, "left")
+    else:
+        left += 2 * _send(g, T, topo, core, "xq", "xs", own, own, NC, [me["partner"]], "ar%d" % rank, "left")
+        left += 2 * _send(g, T, topo, core, "xq", "xs", own, own, NC, me["serve"], "ar%d" % rank, "left")
+        g.wait_ge(S["ar%d" % pj], arrives(pj))
+        left += 2 * _send(g, T, topo, core, "xq", "xs", pj * NC, pj * NC, NC, me["serve"], "ar%d" % pj, "left")
+    g.wait_ge(S.qh, 1)
+    prev = cores[(rank - 1) % N]
+    nxt = cores[(rank + 1) % N]
+    lefth = 2 * _send(g, T, topo, core, "hq", "hs", 0, NC, NC, [prev], "arh", "lefth")
+
+    g.sync.wait_ge(S.left, left)
+    g.sync.dma_start(T.w2b[:], T.w2[:]).then_inc(S.ldw2, 16)
+    g.sync.wait_ge(S.sc, 4)
+    g.sync.wait_ge(S.lefth, lefth)
+    g.sync.dma_start(T.h[:], T.hb[:]).then_inc(S.sth, 16)
+    g.sync.wait_ge(S.cy, 1)
+    g.sync.dma_start(T.y[:], T.yb[:]).then_inc(S.sty, 16)
+    g.sync.wait_ge(S.sth, 16)
+    g.sync.wait_ge(S.sty, 16)
+
+    near = [plan[c]["rank"] for c in me["from"]]
+    far = [plan[plan[c]["partner"]]["rank"] for c in me["from"]]
+    if USE_HELPER:
+        order = [rank] + near + [pj] + far
+    else:
+        order = [rank, pj] + near + far
+
+    def bank(idx, i):
+        b = 2 * (idx % 3) + i
+        return T.ps[:, 512 * b:512 * b + NC]
+
+    te = g.tensor
+    for idx, j in enumerate(order):
+        if idx == 0:
+            te.wait_ge(S.qx, 1)
+            te.wait_ge(S.qw1, 2)
+        else:
+            te.wait_ge(S["ar%d" % j], arrives(j))
+        for i in range(2):
+            if idx == 3:
+                te.wait_ge(S["seed%d" % i], 1)
+            elif idx > 3:
+                te.wait_ge(S["ch%d" % (2 * i)], idx - 3)
+                te.wait_ge(S["ch%d" % (2 * i + 1)], idx - 3)
+            te.matmul_mx(bank(idx, i), T.w1q[:, NC * i:NC * i + NC], T.w1s[:, NC * i:NC * i + NC],
+                         T.xq[:, NC * j:NC * j + NC], T.xs[:, NC * j:NC * j + NC], True, True).then_inc(S["mm%d_%d" % (idx, i)], 1)
+    yps = T.ps[:, 512 * 6:512 * 6 + NC]
+    te.wait_ge(S.qh, 1)
+    te.wait_ge(S.qw2, 2)
+    te.matmul_mx(yps, T.w2q[:, 0:NC], T.w2s[:, 0:NC], T.hq[:, 0:NC], T.hs[:, 0:NC], True, False)
+    te.wait_ge(S.arh, 2 * _bits(topo.mask(nxt, core)))
+    te.matmul_mx(yps, T.w2q[:, NC:2 * NC], T.w2s[:, NC:2 * NC], T.hq[:, NC:2 * NC], T.hs[:, NC:2 * NC], False, True).then_inc(S.my, 1)
+
+    ac = g.scalar
+    for i in range(2):
+        ac.wait_ge(S["mm0_%d" % i], 1)
+        ac.activation(T.seed[:, NC * i:NC * i + NC], bank(0, i), ActivationFunctionType.Copy).then_inc(S["seed%d" % i], 1)
+    for c in range(3):
+        ac.wait_ge(S["ch%d" % c], N - 1)
+        ac.activation(T.hb[:, c:512:4], T.run[:, NC * c:NC * c + NC], ActivationFunctionType.Copy, scale=SCALE).then_inc(S.sc, 1)
+
+    ve = g.vector
+    ve.wait_ge(S.ldx, 16)
+    ve.quantize_mx(T.xq[:, own:own + NC], T.xs[:, own:own + NC], T.xb[:]).then_inc(S.qx, 1)
+    ve.wait_ge(S.ldw1, 16)
+    for i in range(2):
+        ve.quantize_mx(T.w1q[:, NC * i:NC * i + NC], T.w1s[:, NC * i:NC * i + NC], T.w1b[:, 512 * i:512 * i + 512]).then_inc(S.qw1, 1)
+    for idx in range(1, N):
+        for i in range(2):
+            ve.wait_ge(S["mm%d_%d" % (idx, i)], 1)
+            for k, op in enumerate((AluOpType.max, AluOpType.min)):
+                c = 2 * i + k
+                acc = T.run[:, NC * c:NC * c + NC]
+                if idx == 1:
+                    ve.wait_ge(S["seed%d" % i], 1)
+                    ve.tensor_tensor(acc, bank(idx, i), T.seed[:, NC * i:NC * i + NC], op).then_inc(S["ch%d" % c], 1)
+                else:
+                    ve.wait_ge(S["ch%d" % c], idx - 1)
+                    ve.tensor_tensor(acc, bank(idx, i), acc, op).then_inc(S["ch%d" % c], 1)
+    ve.wait_ge(S.ch3, N - 1)
+    ve.tensor_scalar(T.hb[:, 3:512:4], T.run[:, NC * 3:NC * 4], SCALE, None, AluOpType.mult).then_inc(S.sc, 1)
+    ve.wait_ge(S.sc, 4)
+    ve.quantize_mx(T.hq[:, 0:NC], T.hs[:, 0:NC], T.hb[:]).then_inc(S.qh, 1)
+    ve.wait_ge(S.ldw2, 16)
+    for i in range(2):
+        ve.quantize_mx(T.w2q[:, NC * i:NC * i + NC], T.w2s[:, NC * i:NC * i + NC], T.w2b[:, 512 * i:512 * i + 512]).then_inc(S.qw2, 1)
+    ve.wait_ge(S.my, 1)
+    ve.tensor_copy(T.yb[:], yps).then_inc(S.cy, 1)

@@ -3,9 +3,9 @@ from concourse.mybir import dt, AluOpType, ActivationFunctionType
 
 N = 12
 NC = 128
+HC = NC // 2
 WORLD = 512
 SCALE = 0.043
-USE_HELPER = False
 
 SCRATCH = {
     "xb": ("sbuf", [128, 512], "bfloat16"),
@@ -26,13 +26,20 @@ SCRATCH = {
     "ps": ("psum", [128, 512 * 7], "float32"),
 }
 SEMAPHORES = (["ldx", "ldw1", "ldw2", "qx", "qw1", "qw2", "qh", "arh", "left", "lefth", "seed0", "seed1",
-               "ch0", "ch1", "ch2", "ch3", "sc", "my", "cy", "sth", "sty"]
+               "ch0", "ch1", "ch2", "ch3", "sc", "my", "cy", "sth", "sty", "fd", "hc"]
               + ["ar%d" % j for j in range(N)]
+              + ["pl%d" % j for j in range(N)]
               + ["mm%d_%d" % (k, i) for k in range(N) for i in range(2)])
 
 
 def _bits(m):
     return bin(m).count("1")
+
+
+def _halves(m):
+    e = [b for b in range(m.bit_length()) if (m >> b) & 1]
+    lo = sum(1 << b for b in e[:len(e) // 2])
+    return lo, m & ~lo
 
 
 def _plan(T, topo):
@@ -43,33 +50,40 @@ def _plan(T, topo):
         a, n = rack.index(s), len(rack)
         partner = [c for c in cores if topo.rack(topo.host(c)) != topo.rack(topo.host(s))
                    and topo.may_write(s, c) and topo.chip(c) == topo.chip(s)][0]
-        relay = s
-        if USE_HELPER:
-            relay = [c for c in range(WORLD) if topo.host(c) == topo.host(s) and topo.chip(c) == topo.chip(s)
-                     and topo.die(c) != topo.die(s)][0]
-        plan[s] = {"rank": r, "partner": partner, "relay": relay,
-                   "serve": [rack[(a + k) % n] for k in range(1, n)],
-                   "from": [rack[(a - k) % n] for k in range(1, n)]}
+        helpers = [c for c in range(WORLD) if topo.host(c) == topo.host(s) and topo.chip(c) == topo.chip(s)
+                   and topo.die(c) != topo.die(s)][:2]
+        serve = [rack[(a + k) % n] for k in range(1, n)]
+        plan[s] = {"rank": r, "partner": partner, "helpers": helpers, "serve": serve,
+                   "from": [rack[(a - k) % n] for k in range(1, n)],
+                   "share": [serve[0:2], serve[2:4], serve[4:5]]}
     return plan
 
 
-def _send(g, T, topo, core, qbuf, sbuf, src_col, dst_col, width, dests, rsem, lsem):
-    mask = topo.mask(core, dests[0])
-    for d in dests:
-        mask &= topo.mask(core, d)
+def _transfer(T, topo, core, buf, codes, c0, c1, dests, rsem, mask):
     ids = []
     for d in dests:
         rid, pid = topo.addr(d, core)
         ids.append(DstId(rid=rid, pnc=pid))
-    for kind in range(2):
-        if kind == 0:
-            src = T[qbuf][:, src_col:src_col + width].bitcast(dt.uint8)
-            dst = [T[qbuf][:, dst_col:dst_col + width].bitcast(dt.uint8) for _ in dests]
-        else:
-            src = T[sbuf][:, src_col:src_col + width]
-            dst = [T[sbuf][:, dst_col:dst_col + width] for _ in dests]
-        g.remote_dma_fused([RemoteDMATransfer(dst_ids=ids, dma_engine_mask=mask, remote_sem=T.sem[rsem],
-                                              srcs=[src], dsts=dst)], local_sem=T.sem[lsem])
+    if codes:
+        src = T[buf][:, c0:c1].bitcast(dt.uint8)
+        dst = [T[buf][:, c0:c1].bitcast(dt.uint8) for _ in dests]
+    else:
+        src = T[buf][:, c0:c1]
+        dst = [T[buf][:, c0:c1] for _ in dests]
+    return RemoteDMATransfer(dst_ids=ids, dma_engine_mask=mask, remote_sem=T.sem[rsem], srcs=[src], dsts=dst)
+
+
+def _common(topo, core, dests):
+    mask = topo.mask(core, dests[0])
+    for d in dests:
+        mask &= topo.mask(core, d)
+    return mask
+
+
+def _put(g, T, topo, core, buf, codes, c0, c1, dests, rsem, lsem, mask=None):
+    if mask is None:
+        mask = _common(topo, core, dests)
+    g.remote_dma_fused([_transfer(T, topo, core, buf, codes, c0, c1, dests, rsem, mask)], local_sem=T.sem[lsem])
     return _bits(mask)
 
 
@@ -79,46 +93,65 @@ def rank_program(g, core, T, topo):
     rank = T.rank_of(core)
     S = T.sem
 
+    def cable_masks(s):
+        return _halves(_common(topo, s, plan[plan[s]["partner"]]["helpers"]))
+
+    def feed_mask(s):
+        return _common(topo, s, plan[s]["helpers"]) & ~topo.mask(s, plan[s]["partner"])
+
     if rank is None:
         for s in cores:
             p = plan[s]
-            if p["relay"] == core:
-                j = plan[p["partner"]]["rank"]
-                g.wait_ge(S["ar%d" % j], 2 * _bits(topo.mask(p["partner"], core)))
-                e = _send(g, T, topo, core, "xq", "xs", j * NC, j * NC, NC, p["serve"], "ar%d" % j, "left")
-                g.wait_ge(S.left, 2 * e)
+            if core in p["helpers"]:
+                k = p["helpers"].index(core)
+                r, pj = p["rank"], plan[p["partner"]]["rank"]
+                left = 0
+                g.wait_ge(S.fd, _bits(feed_mask(s)))
+                left += _put(g, T, topo, core, "xq", True, r * NC, r * NC + NC, p["share"][1 + k], "ar%d" % r, "left")
+                g.wait_ge(S.hc, _bits(cable_masks(p["partner"])[k]))
+                c0 = pj * NC + k * HC
+                left += _put(g, T, topo, core, "xq", True, c0, c0 + HC, [s] + p["serve"], "ar%d" % pj, "left")
+                g.wait_ge(S.left, left)
         return
 
     me = plan[core]
     pj = plan[me["partner"]]["rank"]
     own = rank * NC
-
-    def arrives(j):
-        src = cores[j]
-        if src == me["partner"] or topo.rack(topo.host(src)) == topo.rack(topo.host(core)):
-            return 2 * _bits(topo.mask(src, core))
-        return 2 * _bits(topo.mask(plan[plan[src]["partner"]]["relay"], core))
+    off = topo.mask(core, me["partner"])
+    EB = _bits(off)
 
     g.sync.dma_start(T.xb[:], T.x[:]).then_inc(S.ldx, 16)
     g.sync.dma_start(T.w1b[:], T.w1[:]).then_inc(S.ldw1, 16)
+    g.sync.dma_start(T.w2b[:], T.w2[:]).then_inc(S.ldw2, 16)
 
     g.wait_ge(S.qx, 1)
     left = 0
-    if USE_HELPER:
-        left += 2 * _send(g, T, topo, core, "xq", "xs", own, own, NC, [plan[me["partner"]]["relay"]], "ar%d" % rank, "left")
-        left += 2 * _send(g, T, topo, core, "xq", "xs", own, own, NC, me["serve"] + [me["partner"]], "ar%d" % rank, "left")
-    else:
-        left += 2 * _send(g, T, topo, core, "xq", "xs", own, own, NC, [me["partner"]], "ar%d" % rank, "left")
-        left += 2 * _send(g, T, topo, core, "xq", "xs", own, own, NC, me["serve"], "ar%d" % rank, "left")
-        g.wait_ge(S["ar%d" % pj], arrives(pj))
-        left += 2 * _send(g, T, topo, core, "xq", "xs", pj * NC, pj * NC, NC, me["serve"], "ar%d" % pj, "left")
+    far_help = plan[me["partner"]]["helpers"]
+    cm = cable_masks(core)
+    g.remote_dma_fused([_transfer(T, topo, core, "xq", True, own + k * HC, own + k * HC + HC, [far_help[k]], "hc", cm[k])
+                        for k in range(2)], local_sem=S.left)
+    left += _bits(cm[0]) + _bits(cm[1])
+    left += _put(g, T, topo, core, "xq", True, own, own + NC, me["helpers"], "fd", "left", feed_mask(core))
+    left += _put(g, T, topo, core, "xs", False, own, own + NC, [me["partner"]] + me["serve"], "pl%d" % rank, "left")
+    left += _put(g, T, topo, core, "xq", True, own, own + NC, me["share"][0], "ar%d" % rank, "left")
+    g.wait_ge(S["pl%d" % pj], EB)
+    left += _put(g, T, topo, core, "xs", False, pj * NC, pj * NC + NC, me["serve"], "pl%d" % pj, "left")
     g.wait_ge(S.qh, 1)
     prev = cores[(rank - 1) % N]
     nxt = cores[(rank + 1) % N]
-    lefth = 2 * _send(g, T, topo, core, "hq", "hs", 0, NC, NC, [prev], "arh", "lefth")
+    hmask = topo.mask(core, prev)
+    rid, pid = topo.addr(prev, core)
+    lefth = 0
+    for kind in range(2):
+        if kind == 0:
+            src, dst = T.hq[:, 0:NC].bitcast(dt.uint8), T.hq[:, NC:2 * NC].bitcast(dt.uint8)
+        else:
+            src, dst = T.hs[:, 0:NC], T.hs[:, NC:2 * NC]
+        g.remote_dma_fused([RemoteDMATransfer(dst_ids=[DstId(rid=rid, pnc=pid)], dma_engine_mask=hmask, remote_sem=S.arh,
+                                              srcs=[src], dsts=[dst])], local_sem=S.lefth)
+        lefth += _bits(hmask)
+    g.wait_ge(S.left, left)
 
-    g.sync.wait_ge(S.left, left)
-    g.sync.dma_start(T.w2b[:], T.w2[:]).then_inc(S.ldw2, 16)
     g.sync.wait_ge(S.sc, 4)
     g.sync.wait_ge(S.lefth, lefth)
     g.sync.dma_start(T.h[:], T.hb[:]).then_inc(S.sth, 16)
@@ -127,12 +160,12 @@ def rank_program(g, core, T, topo):
     g.sync.wait_ge(S.sth, 16)
     g.sync.wait_ge(S.sty, 16)
 
-    near = [plan[c]["rank"] for c in me["from"]]
+    near = [plan[me["from"][k]]["rank"] for k in (0, 1, 2, 4, 3)]
     far = [plan[plan[c]["partner"]]["rank"] for c in me["from"]]
-    if USE_HELPER:
-        order = [rank] + near + [pj] + far
-    else:
-        order = [rank, pj] + near + far
+    order = [rank] + near + [pj] + far
+    codes_in = {j: EB for j in near}
+    for j in [pj] + far:
+        codes_in[j] = 2 * EB
 
     def bank(idx, i):
         b = 2 * (idx % 3) + i
@@ -144,7 +177,8 @@ def rank_program(g, core, T, topo):
             te.wait_ge(S.qx, 1)
             te.wait_ge(S.qw1, 2)
         else:
-            te.wait_ge(S["ar%d" % j], arrives(j))
+            te.wait_ge(S["pl%d" % j], EB)
+            te.wait_ge(S["ar%d" % j], codes_in[j])
         for i in range(2):
             if idx == 3:
                 te.wait_ge(S["seed%d" % i], 1)
@@ -174,6 +208,9 @@ def rank_program(g, core, T, topo):
     ve.wait_ge(S.ldw1, 16)
     for i in range(2):
         ve.quantize_mx(T.w1q[:, NC * i:NC * i + NC], T.w1s[:, NC * i:NC * i + NC], T.w1b[:, 512 * i:512 * i + 512]).then_inc(S.qw1, 1)
+    ve.wait_ge(S.ldw2, 16)
+    for i in range(2):
+        ve.quantize_mx(T.w2q[:, NC * i:NC * i + NC], T.w2s[:, NC * i:NC * i + NC], T.w2b[:, 512 * i:512 * i + 512]).then_inc(S.qw2, 1)
     for idx in range(1, N):
         for i in range(2):
             ve.wait_ge(S["mm%d_%d" % (idx, i)], 1)
@@ -190,8 +227,5 @@ def rank_program(g, core, T, topo):
     ve.tensor_scalar(T.hb[:, 3:512:4], T.run[:, NC * 3:NC * 4], SCALE, None, AluOpType.mult).then_inc(S.sc, 1)
     ve.wait_ge(S.sc, 4)
     ve.quantize_mx(T.hq[:, 0:NC], T.hs[:, 0:NC], T.hb[:]).then_inc(S.qh, 1)
-    ve.wait_ge(S.ldw2, 16)
-    for i in range(2):
-        ve.quantize_mx(T.w2q[:, NC * i:NC * i + NC], T.w2s[:, NC * i:NC * i + NC], T.w2b[:, 512 * i:512 * i + 512]).then_inc(S.qw2, 1)
     ve.wait_ge(S.my, 1)
     ve.tensor_copy(T.yb[:], yps).then_inc(S.cy, 1)

from concourse.bass import DstId, RemoteDMATransfer
from concourse.mybir import dt, AluOpType, ActivationFunctionType

N = 12
NC = 128
HC = NC // 2
WORLD = 512
SCALE = 0.043

SCRATCH = {
    "xb": ("sbuf", [128, 512], "bfloat16"),
    "w1b": ("sbuf", [128, 1024], "bfloat16"),
    "w2b": ("sbuf", [128, 1024], "bfloat16"),
    "xq": ("sbuf", [128, N * NC], "float8_e4m3fn_x4"),
    "xs": ("sbuf", [128, N * NC], "uint8"),
    "w1q": ("sbuf", [128, 256], "float8_e4m3fn_x4"),
    "w1s": ("sbuf", [128, 256], "uint8"),
    "w2q": ("sbuf", [128, 256], "float8_e4m3fn_x4"),
    "w2s": ("sbuf", [128, 256], "uint8"),
    "hb": ("sbuf", [128, 512], "bfloat16"),
    "hq": ("sbuf", [128, 256], "float8_e4m3fn_x4"),
    "hs": ("sbuf", [128, 256], "uint8"),
    "seed": ("sbuf", [128, 256], "float32"),
    "run": ("sbuf", [128, 512], "float32"),
    "yb": ("sbuf", [128, 128], "float32"),
    "ps": ("psum", [128, 512 * 7], "float32"),
}
SEMAPHORES = (["ldx", "ldw1", "ldw2", "qx", "qw1", "qw2", "qh", "arh", "left", "lefth", "seed0", "seed1",
               "ch0", "ch1", "ch2", "ch3", "sc", "my", "cy", "sth", "sty", "fd", "hc"]
              + ["ar%d" % j for j in range(N)]
              + ["pl%d" % j for j in range(N)]
              + ["mm%d_%d" % (k, i) for k in range(N) for i in range(2)])


def _bits(m):
    return bin(m).count("1")


def _halves(m):
    e = [b for b in range(m.bit_length()) if (m >> b) & 1]
    lo = sum(1 << b for b in e[:len(e) // 2])
    return lo, m & ~lo


def _plan(T, topo):
    cores = list(T.cores)
    plan = {}
    for r, s in enumerate(cores):
        rack = [c for c in cores if topo.rack(topo.host(c)) == topo.rack(topo.host(s))]
        a, n = rack.index(s), len(rack)
        partner = [c for c in cores if topo.rack(topo.host(c)) != topo.rack(topo.host(s))
                   and topo.may_write(s, c) and topo.chip(c) == topo.chip(s)][0]
        helpers = [c for c in range(WORLD) if topo.host(c) == topo.host(s) and topo.chip(c) == topo.chip(s)
                   and topo.die(c) != topo.die(s)][:2]
        serve = [rack[(a + k) % n] for k in range(1, n)]
        plan[s] = {"rank": r, "partner": partner, "helpers": helpers, "serve": serve,
                   "from": [rack[(a - k) % n] for k in range(1, n)],
                   "share": [serve[0:2], serve[2:4], serve[4:5]]}
    return plan


def _transfer(T, topo, core, buf, codes, c0, c1, dests, rsem, mask):
    ids = []
    for d in dests:
        rid, pid = topo.addr(d, core)
        ids.append(DstId(rid=rid, pnc=pid))
    if codes:
        src = T[buf][:, c0:c1].bitcast(dt.uint8)
        dst = [T[buf][:, c0:c1].bitcast(dt.uint8) for _ in dests]
    else:
        src = T[buf][:, c0:c1]
        dst = [T[buf][:, c0:c1] for _ in dests]
    return RemoteDMATransfer(dst_ids=ids, dma_engine_mask=mask, remote_sem=T.sem[rsem], srcs=[src], dsts=dst)


def _common(topo, core, dests):
    mask = topo.mask(core, dests[0])
    for d in dests:
        mask &= topo.mask(core, d)
    return mask


def _put(g, T, topo, core, buf, codes, c0, c1, dests, rsem, lsem, mask=None):
    if mask is None:
        mask = _common(topo, core, dests)
    g.remote_dma_fused([_transfer(T, topo, core, buf, codes, c0, c1, dests, rsem, mask)], local_sem=T.sem[lsem])
    return _bits(mask)


def rank_program(g, core, T, topo):
    plan = _plan(T, topo)
    cores = list(T.cores)
    rank = T.rank_of(core)
    S = T.sem

    def cable_masks(s):
        return _halves(_common(topo, s, plan[plan[s]["partner"]]["helpers"]))

    def feed_mask(s):
        return _common(topo, s, plan[s]["helpers"]) & ~topo.mask(s, plan[s]["partner"])

    if rank is None:
        for s in cores:
            p = plan[s]
            if core in p["helpers"]:
                k = p["helpers"].index(core)
                r, pj = p["rank"], plan[p["partner"]]["rank"]
                left = 0
                g.wait_ge(S.fd, _bits(feed_mask(s)))
                left += _put(g, T, topo, core, "xq", True, r * NC, r * NC + NC, p["share"][1 + k], "ar%d" % r, "left")
                g.wait_ge(S.hc, _bits(cable_masks(p["partner"])[k]))
                c0 = pj * NC + k * HC
                left += _put(g, T, topo, core, "xq", True, c0, c0 + HC, [s] + p["serve"], "ar%d" % pj, "left")
                g.wait_ge(S.left, left)
        return

    me = plan[core]
    pj = plan[me["partner"]]["rank"]
    own = rank * NC
    off = topo.mask(core, me["partner"])
    EB = _bits(off)

    g.sync.dma_start(T.xb[:], T.x[:]).then_inc(S.ldx, 16)
    g.sync.dma_start(T.w1b[:], T.w1[:]).then_inc(S.ldw1, 16)
    g.sync.dma_start(T.w2b[:], T.w2[:]).then_inc(S.ldw2, 16)

    g.wait_ge(S.qx, 1)
    left = 0
    far_help = plan[me["partner"]]["helpers"]
    cm = cable_masks(core)
    g.remote_dma_fused([_transfer(T, topo, core, "xq", True, own + k * HC, own + k * HC + HC, [far_help[k]], "hc", cm[k])
                        for k in range(2)], local_sem=S.left)
    left += _bits(cm[0]) + _bits(cm[1])
    left += _put(g, T, topo, core, "xq", True, own, own + NC, me["helpers"], "fd", "left", feed_mask(core))
    left += _put(g, T, topo, core, "xs", False, own, own + NC, [me["partner"]] + me["serve"], "pl%d" % rank, "left")
    left += _put(g, T, topo, core, "xq", True, own, own + NC, me["share"][0], "ar%d" % rank, "left")
    g.wait_ge(S["pl%d" % pj], EB)
    left += _put(g, T, topo, core, "xs", False, pj * NC, pj * NC + NC, me["serve"], "pl%d" % pj, "left")
    g.wait_ge(S.qh, 1)
    prev = cores[(rank - 1) % N]
    nxt = cores[(rank + 1) % N]
    hmask = topo.mask(core, prev)
    rid, pid = topo.addr(prev, core)
    lefth = 0
    for kind in range(2):
        if kind == 0:
            src, dst = T.hq[:, 0:NC].bitcast(dt.uint8), T.hq[:, NC:2 * NC].bitcast(dt.uint8)
        else:
            src, dst = T.hs[:, 0:NC], T.hs[:, NC:2 * NC]
        g.remote_dma_fused([RemoteDMATransfer(dst_ids=[DstId(rid=rid, pnc=pid)], dma_engine_mask=hmask, remote_sem=S.arh,
                                              srcs=[src], dsts=[dst])], local_sem=S.lefth)
        lefth += _bits(hmask)
    g.wait_ge(S.left, left)

    g.sync.wait_ge(S.sc, 4)
    g.sync.wait_ge(S.lefth, lefth)
    g.sync.dma_start(T.h[:], T.hb[:]).then_inc(S.sth, 16)
    g.sync.wait_ge(S.cy, 1)
    g.sync.dma_start(T.y[:], T.yb[:]).then_inc(S.sty, 16)
    g.sync.wait_ge(S.sth, 16)
    g.sync.wait_ge(S.sty, 16)

    near = [plan[me["from"][k]]["rank"] for k in (0, 1, 2, 4, 3)]
    far = [plan[plan[c]["partner"]]["rank"] for c in me["from"]]
    order = [rank] + near + [pj] + far
    codes_in = {j: EB for j in near}
    for j in [pj] + far:
        codes_in[j] = 2 * EB

    def bank(idx, i):
        b = 2 * (idx % 3) + i
        return T.ps[:, 512 * b:512 * b + NC]

    te = g.tensor
    for idx, j in enumerate(order):
        if idx == 0:
            te.wait_ge(S.qx, 1)
            te.wait_ge(S.qw1, 2)
        else:
            te.wait_ge(S["pl%d" % j], EB)
            te.wait_ge(S["ar%d" % j], codes_in[j])
        for i in range(2):
            if idx == 3:
                te.wait_ge(S["seed%d" % i], 1)
            elif idx > 3:
                te.wait_ge(S["ch%d" % (2 * i)], idx - 3)
                te.wait_ge(S["ch%d" % (2 * i + 1)], idx - 3)
            te.matmul_mx(bank(idx, i), T.w1q[:, NC * i:NC * i + NC], T.w1s[:, NC * i:NC * i + NC],
                         T.xq[:, NC * j:NC * j + NC], T.xs[:, NC * j:NC * j + NC], True, True).then_inc(S["mm%d_%d" % (idx, i)], 1)
    yps = T.ps[:, 512 * 6:512 * 6 + NC]
    te.wait_ge(S.qh, 1)
    te.wait_ge(S.qw2, 2)
    te.matmul_mx(yps, T.w2q[:, 0:NC], T.w2s[:, 0:NC], T.hq[:, 0:NC], T.hs[:, 0:NC], True, False)
    te.wait_ge(S.arh, 2 * _bits(topo.mask(nxt, core)))
    te.matmul_mx(yps, T.w2q[:, NC:2 * NC], T.w2s[:, NC:2 * NC], T.hq[:, NC:2 * NC], T.hs[:, NC:2 * NC], False, True).then_inc(S.my, 1)

    ac = g.scalar
    for i in range(2):
        ac.wait_ge(S["mm0_%d" % i], 1)
        ac.activation(T.seed[:, NC * i:NC * i + NC], bank(0, i), ActivationFunctionType.Copy).then_inc(S["seed%d" % i], 1)
    for c in range(3):
        ac.wait_ge(S["ch%d" % c], N - 1)
        ac.activation(T.hb[:, c:512:4], T.run[:, NC * c:NC * c + NC], ActivationFunctionType.Copy, scale=SCALE).then_inc(S.sc, 1)

    ve = g.vector
    ve.wait_ge(S.ldx, 16)
    ve.quantize_mx(T.xq[:, own:own + NC], T.xs[:, own:own + NC], T.xb[:]).then_inc(S.qx, 1)
    ve.wait_ge(S.ldw1, 16)
    for i in range(2):
        ve.quantize_mx(T.w1q[:, NC * i:NC * i + NC], T.w1s[:, NC * i:NC * i + NC], T.w1b[:, 512 * i:512 * i + 512]).then_inc(S.qw1, 1)
    ve.wait_ge(S.ldw2, 16)
    for i in range(2):
        ve.quantize_mx(T.w2q[:, NC * i:NC * i + NC], T.w2s[:, NC * i:NC * i + NC], T.w2b[:, 512 * i:512 * i + 512]).then_inc(S.qw2, 1)
    for idx in range(1, N):
        for i in range(2):
            ve.wait_ge(S["mm%d_%d" % (idx, i)], 1)
            for k, op in enumerate((AluOpType.max, AluOpType.min)):
                c = 2 * i + k
                acc = T.run[:, NC * c:NC * c + NC]
                if idx == 1:
                    ve.wait_ge(S["seed%d" % i], 1)
                    ve.tensor_tensor(acc, bank(idx, i), T.seed[:, NC * i:NC * i + NC], op).then_inc(S["ch%d" % c], 1)
                else:
                    ve.wait_ge(S["ch%d" % c], idx - 1)
                    ve.tensor_tensor(acc, bank(idx, i), acc, op).then_inc(S["ch%d" % c], 1)
    ve.wait_ge(S.ch3, N - 1)
    ve.tensor_scalar(T.hb[:, 3:512:4], T.run[:, NC * 3:NC * 4], SCALE, None, AluOpType.mult).then_inc(S.sc, 1)
    ve.wait_ge(S.sc, 4)
    ve.quantize_mx(T.hq[:, 0:NC], T.hs[:, 0:NC], T.hb[:]).then_inc(S.qh, 1)
    ve.wait_ge(S.my, 1)
    ve.tensor_copy(T.yb[:], yps).then_inc(S.cy, 1)
